import numpy as np, ml_dtypes
CORES = [89,94,345,350]
N = 4
import mx_ref
NC, G = 192, 2
C = np.float32(0.043)
WID = [160,128,160,192]
BF = ml_dtypes.bfloat16
def cut(t, i, w=512):
    return t[:, w * i:w * i + w]
def tile(rs):
    return np.stack(rs, axis=2).reshape(128, -1).astype(BF)
def layer(w, X):
    out = []
    for i in range(G):
        for t in range(len(X)):
            p = mx_ref.matmul(mx_ref.quantize(cut(w, len(X) * i + t)), X[t])
            z = p if t == 0 else z + p
        out.append(z)
    return out
def act(Z):
    return [np.maximum(s * z, 0) * C for z in Z for s in (1, -1)]
def setup_inputs(rng):
    def f(*shape):
        return mx_ref.flush((rng.standard_normal(shape, dtype=np.float32) * np.exp2(rng.integers(-2, 3, shape[:-1] + (1,)))).astype(BF))
    return {"x": f(N, 128, 4 * NC), "w1": f(N, 128, G * 512), "w2": f(N, 128, 512)}
def setup_inputs_blocks(rng):
    d = setup_inputs(rng)
    for k in ("x", "w1", "w2"): d[k] = mx_ref.spread(d[k], rng, 2)
    return d
def setup_inputs_wide(rng):
    d = setup_inputs(rng)
    for k in ("x", "w1", "w2"): d[k] = mx_ref.flush((d[k].astype(np.float32) * np.exp2(rng.integers(-6, 7, (N, 1, 1))).astype(np.float32)).astype(BF))
    return d
def reference(x, w1, w2):
    X = [mx_ref.quantize(x[j][:, :4 * WID[j]]) for j in range(N)]
    y = np.full((N, 128, NC), np.nan, np.float32)
    for c in range(N):
        for r in range(N):
            p = mx_ref.matmul(mx_ref.quantize(w2[r]), mx_ref.quantize(tile(act(layer(w1[r], [X[c]])))))
            z = p if r == 0 else z + p
        y[c][:, :WID[c]] = z
    return {"y": y}

@@ -1,0 +1,209 @@
+from concourse.mybir import dt, AluOpType, ActivationFunctionType
+
+WX = 192
+WW = 384
+TW = 128
+NCORES = 512
+NHOSTS = 4
+ALPHA = 0.043
+
+SCRATCH = {
+    "xb": ("sbuf", [128, 4 * WX], "bfloat16"),
+    "wb": ("sbuf", [128, 4 * WW], "bfloat16"),
+    "xq": ("sbuf", [128, WX], "float8_e4m3fn_x4"), "xs": ("sbuf", [128, WX], "uint8"),
+    "wq": ("sbuf", [128, WW], "float8_e4m3fn_x4"), "ws": ("sbuf", [128, WW], "uint8"),
+    "pq": ("sbuf", [128, WW], "float8_e4m3fn_x4"), "ps": ("sbuf", [128, WW], "uint8"),
+    "rq": ("sbuf", [128, WX], "float8_e4m3fn_x4"), "rs": ("sbuf", [128, WX], "uint8"),
+    "yp": ("sbuf", [128, WX], "float32"),
+    "yr": ("sbuf", [128, WX], "float32"),
+    "yl": ("sbuf", [128, WX], "float32"),
+    "yo": ("sbuf", [128, WX], "float32"),
+}
+for _k in ("lo", "ro", "rp", "lp"):
+    SCRATCH["h_" + _k] = ("sbuf", [128, 4 * WX], "bfloat16")
+    SCRATCH["hq_" + _k] = ("sbuf", [128, WX], "float8_e4m3fn_x4")
+    SCRATCH["hs_" + _k] = ("sbuf", [128, WX], "uint8")
+for _k in ("zl0", "zl1", "zo0", "zo1", "zp0", "zp1", "yloc", "yrem"):
+    SCRATCH[_k] = ("psum", [128, 512], "float32")
+
+SEMAPHORES = ["xl", "wl", "xqd", "wqd", "sent", "xarr", "parr", "yarr", "rx", "ry", "yrd", "yld", "ypd", "yod", "st", "v2s"]
+for _k in ("lo", "ro", "rp", "lp"):
+    SEMAPHORES += ["z0" + _k, "z1" + _k, "av" + _k, "as" + _k, "q" + _k]
+
+
+def _bits(mask):
+    return bin(mask).count("1")
+
+
+def _roles(T, topo):
+    cores = list(T.cores)
+    lanes, relays = [], {}
+    for c in cores:
+        peer = [k for k, d in enumerate(cores) if d != c and topo.host(d) == topo.host(c)][0]
+        mate = [k for k, d in enumerate(cores) if topo.host(d) != topo.host(c) and topo.die(d) == topo.die(c)][0]
+        lanes.append((peer, mate))
+    for r, c in enumerate(cores):
+        m = cores[lanes[r][1]]
+        for h in range(NHOSTS):
+            if h in (topo.host(c), topo.host(m)):
+                continue
+            near = [d for d in range(NCORES)
+                    if topo.host(d) == h and topo.chip(d) == topo.chip(c) and topo.die(d) == topo.die(c)]
+            if topo.rack(h) != topo.rack(topo.host(c)):
+                relays[(r, "cable")] = near[0]
+            else:
+                relays[(r, "switch")] = near[-1]
+    return lanes, relays
+
+
+def rank_program(g, core, T, topo):
+    wid = T.tables["WID"]
+    cores = list(T.cores)
+    if topo.chip(core) not in [topo.chip(c) for c in cores]:
+        return
+    lanes, relays = _roles(T, topo)
+    s = T.sem
+
+    def send(dst, out, in_, rsem, mask):
+        rid, pid = topo.addr(dst, core)
+        g.remote_dma(out, in_, rsem, s.sent, pid, rid, mask)
+        return _bits(mask)
+
+    rank = T.rank_of(core)
+    if rank is None:
+        n = 0
+        for (r, way), relay in relays.items():
+            if relay != core:
+                continue
+            mate = lanes[r][1]
+            dst, src = cores[mate], cores[r]
+            m, came = topo.mask(core, dst), _bits(topo.mask(src, core))
+            g.wait_ge(s.rx, came)
+            if way == "cable":
+                v = T.rq[:, 0:wid[r]].bitcast(dt.uint8)
+                n += send(dst, v, v, s.xarr, m)
+                g.wait_ge(s.ry, came)
+                n += send(dst, T.yl[:, 0:wid[mate]], T.yr[:, 0:wid[mate]], s.yarr, m)
+            else:
+                n += send(dst, T.rs[:, 0:wid[r]], T.rs[:, 0:wid[r]], s.xarr, m)
+        if n:
+            g.wait_ge(s.sent, n)
+        return
+
+    peer, mate = lanes[rank]
+    nl, nr = wid[rank], wid[mate]
+    rc, rw = relays[(rank, "cable")], relays[(rank, "switch")]
+    pc = cores[peer]
+    inc, inw = relays[(mate, "cable")], relays[(mate, "switch")]
+    off = topo.mask(core, rc)
+    on = topo.mask(core, pc) & ~off
+    y_need = _bits(topo.mask(inc, core))
+    x_need = y_need + _bits(topo.mask(inw, core))
+    p_need = 2 * _bits(on)
+
+    g.sync.dma_start(T.xb[:, 0:4 * nl], T.x[:, 0:4 * nl]).then_inc(s.xl, 16)
+    g.sync.dma_start(T.wb[:, 0:8 * TW], T.w1[:, :]).then_inc(s.wl, 16)
+    g.sync.dma_start(T.wb[:, 8 * TW:12 * TW], T.w2[:, :]).then_inc(s.wl, 16)
+
+    n = 0
+    g.wait_ge(s.xqd, 1)
+    n += send(rc, T.rq[:, 0:nl].bitcast(dt.uint8), T.xq[:, 0:nl].bitcast(dt.uint8), s.rx, off)
+    n += send(rw, T.rs[:, 0:nl], T.xs[:, 0:nl], s.rx, topo.mask(core, rw))
+    g.wait_ge(s.wqd, 1)
+    n += send(pc, T.pq[:, :].bitcast(dt.uint8), T.wq[:, :].bitcast(dt.uint8), s.parr, on)
+    n += send(pc, T.ps[:, :], T.ws[:, :], s.parr, on)
+    g.wait_ge(s.ypd, 1)
+    n += send(rc, T.yr[:, 0:nr], T.yp[:, 0:nr], s.ry, off)
+    g.wait_ge(s.sent, n)
+
+    te = g.tensor
+
+    def mm(out, n, wq, ws, i, xq, xs, start=True, stop=True):
+        a, b = TW * i, TW * i + TW
+        return te.matmul_mx(out[:, 0:n], wq[:, a:b], ws[:, a:b], xq[:, 0:n], xs[:, 0:n], start, stop)
+
+    te.wait_ge(s.xqd, 1)
+    te.wait_ge(s.wqd, 1)
+    mm(T.zl0, nl, T.wq, T.ws, 0, T.xq, T.xs).then_inc(s.z0lo, 1)
+    mm(T.zl1, nl, T.wq, T.ws, 1, T.xq, T.xs).then_inc(s.z1lo, 1)
+    te.wait_ge(s.qlo, 1)
+    mm(T.yloc, nl, T.wq, T.ws, 2, T.hq_lo, T.hs_lo, True, False)
+    te.wait_ge(s.xarr, x_need)
+    mm(T.zo0, nr, T.wq, T.ws, 0, T.rq, T.rs).then_inc(s.z0ro, 1)
+    mm(T.zo1, nr, T.wq, T.ws, 1, T.rq, T.rs).then_inc(s.z1ro, 1)
+    te.wait_ge(s.parr, p_need)
+    mm(T.zp0, nr, T.pq, T.ps, 0, T.rq, T.rs).then_inc(s.z0rp, 1)
+    mm(T.zp1, nr, T.pq, T.ps, 1, T.rq, T.rs).then_inc(s.z1rp, 1)
+    te.wait_ge(s.qro, 1)
+    mm(T.yrem, nr, T.wq, T.ws, 2, T.hq_ro, T.hs_ro, True, False)
+    te.wait_ge(s.qrp, 1)
+    mm(T.yrem, nr, T.pq, T.ps, 2, T.hq_rp, T.hs_rp, False, True).then_inc(s.yrd, 1)
+    mm(T.zl0, nl, T.pq, T.ps, 0, T.xq, T.xs).then_inc(s.z0lp, 1)
+    mm(T.zl1, nl, T.pq, T.ps, 1, T.xq, T.xs).then_inc(s.z1lp, 1)
+    te.wait_ge(s.qlp, 1)
+    mm(T.yloc, nl, T.pq, T.ps, 2, T.hq_lp, T.hs_lp, False, True).then_inc(s.yld, 1)
+
+    ve, sc = g.vector, g.scalar
+
+    def act_s(h, b, n, z, sem):
+        sc.activation(h[:, b:4 * n:4], z[:, 0:n], ActivationFunctionType.Relu,
+                      scale=-ALPHA if b % 2 else ALPHA).then_inc(sem, 1)
+
+    def act_v(h, b, n, z, sem):
+        ve.tensor_scalar(h[:, b:4 * n:4], z[:, 0:n], -ALPHA if b % 2 else ALPHA, 0.0,
+                         AluOpType.mult, AluOpType.max).then_inc(sem, 1)
+
+    def quant(k, n):
+        ve.quantize_mx(T["hq_" + k][:, 0:n], T["hs_" + k][:, 0:n], T["h_" + k][:, 0:4 * n]).then_inc(T.sem["q" + k], 1)
+
+    sc.wait_ge(s.z0lo, 1)
+    act_s(T.h_lo, 0, nl, T.zl0, s.aslo)
+    act_s(T.h_lo, 1, nl, T.zl0, s.aslo)
+    sc.wait_ge(s.z0ro, 1)
+    act_s(T.h_ro, 0, nr, T.zo0, s.asro)
+    act_s(T.h_ro, 1, nr, T.zo0, s.asro)
+    sc.wait_ge(s.v2s, 1)
+    act_s(T.h_ro, 2, nr, T.zo1, s.asro)
+    sc.wait_ge(s.z1rp, 1)
+    act_s(T.h_rp, 2, nr, T.zp1, s.asrp)
+    act_s(T.h_rp, 3, nr, T.zp1, s.asrp)
+    sc.wait_ge(s.yrd, 1)
+    sc.activation(T.yp[:, 0:nr], T.yrem[:, 0:nr], ActivationFunctionType.Copy).then_inc(s.ypd, 1)
+    sc.wait_ge(s.z0lp, 1)
+    act_s(T.h_lp, 0, nl, T.zl0, s.aslp)
+    act_s(T.h_lp, 1, nl, T.zl0, s.aslp)
+
+    ve.wait_ge(s.xl, 16)
+    ve.quantize_mx(T.xq[:, 0:nl], T.xs[:, 0:nl], T.xb[:, 0:4 * nl]).then_inc(s.xqd, 1)
+    ve.wait_ge(s.wl, 32)
+    ve.quantize_mx(T.wq[:, :], T.ws[:, :], T.wb[:, :]).then_inc(s.wqd, 1)
+    ve.wait_ge(s.z1lo, 1)
+    act_v(T.h_lo, 2, nl, T.zl1, s.avlo)
+    act_v(T.h_lo, 3, nl, T.zl1, s.avlo)
+    ve.wait_ge(s.aslo, 2)
+    ve.wait_ge(s.avlo, 2)
+    quant("lo", nl)
+    ve.wait_ge(s.z1ro, 1)
+    act_v(T.h_ro, 3, nr, T.zo1, s.v2s)
+    ve.wait_ge(s.z0rp, 1)
+    act_v(T.h_rp, 0, nr, T.zp0, s.avrp)
+    ve.wait_ge(s.asro, 3)
+    ve.wait_ge(s.v2s, 1)
+    quant("ro", nr)
+    act_v(T.h_rp, 1, nr, T.zp0, s.avrp)
+    ve.wait_ge(s.asrp, 2)
+    ve.wait_ge(s.avrp, 2)
+    quant("rp", nr)
+    ve.wait_ge(s.z1lp, 1)
+    act_v(T.h_lp, 2, nl, T.zl1, s.avlp)
+    act_v(T.h_lp, 3, nl, T.zl1, s.avlp)
+    ve.wait_ge(s.aslp, 2)
+    ve.wait_ge(s.avlp, 2)
+    quant("lp", nl)
+    ve.wait_ge(s.yld, 1)
+    ve.wait_ge(s.yarr, y_need)
+    ve.tensor_tensor(T.yo[:, 0:nl], T.yloc[:, 0:nl], T.yl[:, 0:nl], AluOpType.add).then_inc(s.yod, 1)
+
+    g.sync.wait_ge(s.yod, 1)
+    g.sync.dma_start(T.y[:, 0:nl], T.yo[:, 0:nl]).then_inc(s.st, 16)
+    g.sync.wait_ge(s.st, 16)

@@ -1,11 +1,14 @@
+from concourse.bass import DstId, RemoteDMATransfer
 from concourse.mybir import dt, AluOpType, ActivationFunctionType
 
 WX = 192
 WW = 384
 TW = 128
 NCORES = 512
-NHOSTS = 4
 ALPHA = 0.043
+
+X_CALLS = [[("s", 0, .5, "cable"), ("s", .5, 1, "switch")], [("q", 0, .5, "cable"), ("q", .5, 1, "switch")]]
+Y_CALLS = [[("y", 0, .5, "cable"), ("y", .5, 1, "switch")]]
 
 SCRATCH = {
     "xb": ("sbuf", [128, 4 * WX], "bfloat16"),
@@ -15,7 +18,6 @@ SCRATCH = {
     "pq": ("sbuf", [128, WW], "float8_e4m3fn_x4"), "ps": ("sbuf", [128, WW], "uint8"),
     "rq": ("sbuf", [128, WX], "float8_e4m3fn_x4"), "rs": ("sbuf", [128, WX], "uint8"),
     "yp": ("sbuf", [128, WX], "float32"),
-    "yr": ("sbuf", [128, WX], "float32"),
     "yl": ("sbuf", [128, WX], "float32"),
     "yo": ("sbuf", [128, WX], "float32"),
 }
@@ -26,7 +28,8 @@ for _k in ("lo", "ro", "rp", "lp"):
 for _k in ("zl0", "zl1", "zo0", "zo1", "zp0", "zp1", "yloc", "yrem"):
     SCRATCH[_k] = ("psum", [128, 512], "float32")
 
-SEMAPHORES = ["xl", "wl", "xqd", "wqd", "sent", "xarr", "parr", "yarr", "rx", "ry", "yrd", "yld", "ypd", "yod", "st", "v2s"]
+SEMAPHORES = ["xl", "wl", "xqd", "wqd", "sent", "xarr", "parr", "yarr", "yrd", "yld", "ypd", "yod", "st", "v2s"]
+SEMAPHORES += ["r%d" % _k for _k in range(8)]
 for _k in ("lo", "ro", "rp", "lp"):
     SEMAPHORES += ["z0" + _k, "z1" + _k, "av" + _k, "as" + _k, "q" + _k]
 
@@ -35,25 +38,24 @@ def _bits(mask):
     return bin(mask).count("1")
 
 
+def _split(mask, k):
+    e = [1 << i for i in range(16) if mask >> i & 1]
+    w = len(e) // k
+    return [sum(e[j * w:j * w + w]) for j in range(k)]
+
+
 def _roles(T, topo):
     cores = list(T.cores)
-    lanes, relays = [], {}
+    lanes = []
     for c in cores:
         peer = [k for k, d in enumerate(cores) if d != c and topo.host(d) == topo.host(c)][0]
         mate = [k for k, d in enumerate(cores) if topo.host(d) != topo.host(c) and topo.die(d) == topo.die(c)][0]
-        lanes.append((peer, mate))
-    for r, c in enumerate(cores):
-        m = cores[lanes[r][1]]
-        for h in range(NHOSTS):
-            if h in (topo.host(c), topo.host(m)):
-                continue
-            near = [d for d in range(NCORES)
-                    if topo.host(d) == h and topo.chip(d) == topo.chip(c) and topo.die(d) == topo.die(c)]
-            if topo.rack(h) != topo.rack(topo.host(c)):
-                relays[(r, "cable")] = near[0]
-            else:
-                relays[(r, "switch")] = near[-1]
-    return lanes, relays
+        near = [d for d in range(NCORES) if topo.chip(d) == topo.chip(c) and topo.die(d) == topo.die(c)
+                and topo.host(d) not in (topo.host(c), topo.host(cores[mate]))]
+        cable = [d for d in near if topo.rack(topo.host(d)) != topo.rack(topo.host(c))][0]
+        switch = [d for d in near if topo.rack(topo.host(d)) == topo.rack(topo.host(c))][-1]
+        lanes.append((peer, mate, {"cable": cable, "switch": switch}))
+    return lanes
 
 
 def rank_program(g, core, T, topo):
@@ -61,7 +63,7 @@ def rank_program(g, core, T, topo):
     cores = list(T.cores)
     if topo.chip(core) not in [topo.chip(c) for c in cores]:
         return
-    lanes, relays = _roles(T, topo)
+    lanes = _roles(T, topo)
     s = T.sem
 
     def send(dst, out, in_, rsem, mask):
@@ -69,36 +71,56 @@ def rank_program(g, core, T, topo):
         g.remote_dma(out, in_, rsem, s.sent, pid, rid, mask)
         return _bits(mask)
 
+    def view(kind, src, a, b):
+        if kind == "q":
+            return (T.xq if src else T.rq)[:, a:b].bitcast(dt.uint8)
+        if kind == "s":
+            return (T.xs if src else T.rs)[:, a:b]
+        return (T.yp if src else T.yl)[:, a:b]
+
+    def plan(r):
+        out = []
+        for i, call in enumerate(X_CALLS + Y_CALLS):
+            for j, (kind, lo, hi, way) in enumerate(call):
+                w = wid[lanes[r][1]] if kind == "y" else wid[r]
+                relay = lanes[r][2][way]
+                mask = _split(topo.mask(cores[r], relay), len(call))[j]
+                out.append((i, kind, int(w * lo), int(w * hi), relay, mask, "r%d" % len(out)))
+        return out
+
+    def issue(pieces):
+        if len(pieces) == 1:
+            _, kind, a, b, relay, mask, sem = pieces[0]
+            return send(relay, view(kind, False, a, b), view(kind, True, a, b), T.sem[sem], mask)
+        ts = []
+        for _, kind, a, b, relay, mask, sem in pieces:
+            rid, pid = topo.addr(relay, core)
+            ts.append(RemoteDMATransfer(dst_ids=[DstId(rid=rid, pnc=pid)], dma_engine_mask=mask, remote_sem=T.sem[sem],
+                                        src=view(kind, True, a, b), dst=view(kind, False, a, b)))
+        g.remote_dma_fused(ts, local_sem=s.sent)
+        return sum(_bits(p[5]) for p in pieces)
+
     rank = T.rank_of(core)
     if rank is None:
         n = 0
-        for (r, way), relay in relays.items():
-            if relay != core:
-                continue
-            mate = lanes[r][1]
-            dst, src = cores[mate], cores[r]
-            m, came = topo.mask(core, dst), _bits(topo.mask(src, core))
-            g.wait_ge(s.rx, came)
-            if way == "cable":
-                v = T.rq[:, 0:wid[r]].bitcast(dt.uint8)
-                n += send(dst, v, v, s.xarr, m)
-                g.wait_ge(s.ry, came)
-                n += send(dst, T.yl[:, 0:wid[mate]], T.yr[:, 0:wid[mate]], s.yarr, m)
-            else:
-                n += send(dst, T.rs[:, 0:wid[r]], T.rs[:, 0:wid[r]], s.xarr, m)
+        for r in range(len(cores)):
+            for _, kind, a, b, relay, mask, sem in plan(r):
+                if relay == core:
+                    dst = cores[lanes[r][1]]
+                    g.wait_ge(T.sem[sem], _bits(mask))
+                    v = view(kind, False, a, b)
+                    n += send(dst, v, v, s.yarr if kind == "y" else s.xarr, topo.mask(core, dst))
         if n:
             g.wait_ge(s.sent, n)
         return
 
-    peer, mate = lanes[rank]
+    peer, mate, relays = lanes[rank]
     nl, nr = wid[rank], wid[mate]
-    rc, rw = relays[(rank, "cable")], relays[(rank, "switch")]
     pc = cores[peer]
-    inc, inw = relays[(mate, "cable")], relays[(mate, "switch")]
-    off = topo.mask(core, rc)
-    on = topo.mask(core, pc) & ~off
-    y_need = _bits(topo.mask(inc, core))
-    x_need = y_need + _bits(topo.mask(inw, core))
+    on = topo.mask(core, pc) & ~topo.mask(core, relays["cable"])
+    mine, his = plan(rank), plan(mate)
+    x_need = sum(_bits(topo.mask(p[4], core)) for p in his if p[1] != "y")
+    y_need = sum(_bits(topo.mask(p[4], core)) for p in his if p[1] == "y")
     p_need = 2 * _bits(on)
 
     g.sync.dma_start(T.xb[:, 0:4 * nl], T.x[:, 0:4 * nl]).then_inc(s.xl, 16)
@@ -107,13 +129,14 @@ def rank_program(g, core, T, topo):
 
     n = 0
     g.wait_ge(s.xqd, 1)
-    n += send(rc, T.rq[:, 0:nl].bitcast(dt.uint8), T.xq[:, 0:nl].bitcast(dt.uint8), s.rx, off)
-    n += send(rw, T.rs[:, 0:nl], T.xs[:, 0:nl], s.rx, topo.mask(core, rw))
+    for i in range(len(X_CALLS)):
+        n += issue([p for p in mine if p[0] == i])
     g.wait_ge(s.wqd, 1)
     n += send(pc, T.pq[:, :].bitcast(dt.uint8), T.wq[:, :].bitcast(dt.uint8), s.parr, on)
     n += send(pc, T.ps[:, :], T.ws[:, :], s.parr, on)
     g.wait_ge(s.ypd, 1)
-    n += send(rc, T.yr[:, 0:nr], T.yp[:, 0:nr], s.ry, off)
+    for i in range(len(X_CALLS), len(X_CALLS) + len(Y_CALLS)):
+        n += issue([p for p in mine if p[0] == i])
     g.wait_ge(s.sent, n)
 
     te = g.tensor

@@ -2,36 +2,38 @@ from concourse.bass import DstId, RemoteDMATransfer
 from concourse.mybir import dt, AluOpType, ActivationFunctionType
 
 WX = 192
+WA = 384
 WW = 384
 TW = 128
 NCORES = 512
 ALPHA = 0.043
 
-X_CALLS = [[("s", 0, .5, "cable"), ("s", .5, 1, "switch")], [("q", 0, .5, "cable"), ("q", .5, 1, "switch")]]
-Y_CALLS = [[("y", 0, .5, "cable"), ("y", .5, 1, "switch")]]
-
 SCRATCH = {
     "xb": ("sbuf", [128, 4 * WX], "bfloat16"),
     "wb": ("sbuf", [128, 4 * WW], "bfloat16"),
-    "xq": ("sbuf", [128, WX], "float8_e4m3fn_x4"), "xs": ("sbuf", [128, WX], "uint8"),
+    "xq": ("sbuf", [128, WA], "float8_e4m3fn_x4"), "xs": ("sbuf", [128, WA], "uint8"),
     "wq": ("sbuf", [128, WW], "float8_e4m3fn_x4"), "ws": ("sbuf", [128, WW], "uint8"),
-    "pq": ("sbuf", [128, WW], "float8_e4m3fn_x4"), "ps": ("sbuf", [128, WW], "uint8"),
-    "rq": ("sbuf", [128, WX], "float8_e4m3fn_x4"), "rs": ("sbuf", [128, WX], "uint8"),
+    "rq": ("sbuf", [128, WW], "float8_e4m3fn_x4"), "rs": ("sbuf", [128, WW], "uint8"),
     "yp": ("sbuf", [128, WX], "float32"),
     "yl": ("sbuf", [128, WX], "float32"),
+    "ye": ("sbuf", [128, WX], "float32"),
+    "e0": ("sbuf", [128, WX], "float32"),
+    "e1": ("sbuf", [128, WX], "float32"),
     "yo": ("sbuf", [128, WX], "float32"),
 }
-for _k in ("lo", "ro", "rp", "lp"):
+GROUPS = ("le", "lh", "rp", "ro")
+for _k in GROUPS:
     SCRATCH["h_" + _k] = ("sbuf", [128, 4 * WX], "bfloat16")
     SCRATCH["hq_" + _k] = ("sbuf", [128, WX], "float8_e4m3fn_x4")
     SCRATCH["hs_" + _k] = ("sbuf", [128, WX], "uint8")
-for _k in ("zl0", "zl1", "zo0", "zo1", "zp0", "zp1", "yloc", "yrem"):
+for _k in ("z0", "z1", "z2", "z3", "yle", "ylh", "yrp", "yro"):
     SCRATCH[_k] = ("psum", [128, 512], "float32")
 
-SEMAPHORES = ["xl", "wl", "xqd", "wqd", "sent", "xarr", "parr", "yarr", "yrd", "yld", "ypd", "yod", "st", "v2s"]
-SEMAPHORES += ["r%d" % _k for _k in range(8)]
-for _k in ("lo", "ro", "rp", "lp"):
-    SEMAPHORES += ["z0" + _k, "z1" + _k, "av" + _k, "as" + _k, "q" + _k]
+SEMAPHORES = ["xl", "w1l", "w2l", "xqd", "w1q", "w2q", "sent", "xearr", "w1arr", "w2arr", "xparr", "yarr", "e0arr", "e1arr",
+              "yed", "ypc", "yoc", "ypd", "v1", "v2", "v3", "yod", "yod2", "st", "st2"]
+SEMAPHORES += ["r%d" % _k for _k in range(12)]
+for _k in GROUPS:
+    SEMAPHORES += ["z0" + _k, "z1" + _k, "av" + _k, "as" + _k, "q" + _k, "y" + _k]
 
 
 def _bits(mask):
@@ -40,8 +42,7 @@ def _bits(mask):
 
 def _split(mask, k):
     e = [1 << i for i in range(16) if mask >> i & 1]
-    w = len(e) // k
-    return [sum(e[j * w:j * w + w]) for j in range(k)]
+    return [sum(e[j::k]) for j in range(k)]
 
 
 def _roles(T, topo):
@@ -65,168 +66,253 @@ def rank_program(g, core, T, topo):
         return
     lanes = _roles(T, topo)
     s = T.sem
+    hv = max(range(len(cores)), key=lambda k: wid[k])
+    lt = lanes[hv][1]
+    wa, wh = wid[lt], wid[hv]
+    we = wid[lanes[hv][0]]
+    helpers = (lt, lanes[lt][0])
 
-    def send(dst, out, in_, rsem, mask):
-        rid, pid = topo.addr(dst, core)
-        g.remote_dma(out, in_, rsem, s.sent, pid, rid, mask)
-        return _bits(mask)
-
-    def view(kind, src, a, b):
-        if kind == "q":
-            return (T.xq if src else T.rq)[:, a:b].bitcast(dt.uint8)
-        if kind == "s":
-            return (T.xs if src else T.rs)[:, a:b]
-        return (T.yp if src else T.yl)[:, a:b]
+    def view(kind, src, r, a, b):
+        if kind == "xq":
+            return T.xq[:, a:b].bitcast(dt.uint8)
+        if kind == "xs":
+            return T.xs[:, a:b]
+        if kind[1] == "q":
+            return (T.wq if src else T.rq)[:, a:b].bitcast(dt.uint8)
+        if kind[1] == "s":
+            return (T.ws if src else T.rs)[:, a:b]
+        return (T.ye if src else T.e0 if r == lt else T.e1)[:, a:b]
 
     def plan(r):
+        def halves(a, b):
+            m = (a + b) // 2
+            return [(a, m, "cable"), (m, b, "switch")]
+        calls = []
+        if r == hv:
+            calls += [(k, halves(wa, wh), helpers, "xearr") for k in ("xs", "xq")]
+        mate = (lanes[r][1],)
+        calls += [(k, halves(0, 2 * TW), mate, "w1arr") for k in ("1s", "1q")]
+        calls += [(k, halves(2 * TW, 3 * TW), mate, "w2arr") for k in ("2s", "2q")]
+        if r in helpers:
+            calls += [("ye", halves(0, wh - wa), (hv,), "e0arr" if r == lt else "e1arr")]
         out = []
-        for i, call in enumerate(X_CALLS + Y_CALLS):
-            for j, (kind, lo, hi, way) in enumerate(call):
-                w = wid[lanes[r][1]] if kind == "y" else wid[r]
+        for kind, hs, to, asem in calls:
+            for j, (a, b, way) in enumerate(hs):
                 relay = lanes[r][2][way]
-                mask = _split(topo.mask(cores[r], relay), len(call))[j]
-                out.append((i, kind, int(w * lo), int(w * hi), relay, mask, "r%d" % len(out)))
+                out.append((kind, a, b, relay, _split(topo.mask(cores[r], relay), len(hs))[j], "r%d" % len(out), to, asem))
         return out
-
-    def issue(pieces):
-        if len(pieces) == 1:
-            _, kind, a, b, relay, mask, sem = pieces[0]
-            return send(relay, view(kind, False, a, b), view(kind, True, a, b), T.sem[sem], mask)
-        ts = []
-        for _, kind, a, b, relay, mask, sem in pieces:
-            rid, pid = topo.addr(relay, core)
-            ts.append(RemoteDMATransfer(dst_ids=[DstId(rid=rid, pnc=pid)], dma_engine_mask=mask, remote_sem=T.sem[sem],
-                                        src=view(kind, True, a, b), dst=view(kind, False, a, b)))
-        g.remote_dma_fused(ts, local_sem=s.sent)
-        return sum(_bits(p[5]) for p in pieces)
 
     rank = T.rank_of(core)
     if rank is None:
         n = 0
         for r in range(len(cores)):
-            for _, kind, a, b, relay, mask, sem in plan(r):
+            for kind, a, b, relay, mask, sem, to, asem in plan(r):
                 if relay == core:
-                    dst = cores[lanes[r][1]]
                     g.wait_ge(T.sem[sem], _bits(mask))
-                    v = view(kind, False, a, b)
-                    n += send(dst, v, v, s.yarr if kind == "y" else s.xarr, topo.mask(core, dst))
+                    v = view(kind, False, r, a, b)
+                    out = topo.mask(core, cores[to[0]])
+                    if len(to) == 1:
+                        rid, pid = topo.addr(cores[to[0]], core)
+                        g.remote_dma(v, v, T.sem[asem], s.sent, pid, rid, out)
+                    else:
+                        ids = []
+                        for k in to:
+                            rid, pid = topo.addr(cores[k], core)
+                            ids.append(DstId(rid=rid, pnc=pid))
+                        g.remote_dma_fused([RemoteDMATransfer(dst_ids=ids, dma_engine_mask=out, remote_sem=T.sem[asem],
+                                                              srcs=[v], dsts=[v for k in to])], local_sem=s.sent)
+                    n += _bits(out)
         if n:
             g.wait_ge(s.sent, n)
         return
 
     peer, mate, relays = lanes[rank]
-    nl, nr = wid[rank], wid[mate]
+    heavy = rank in (hv, lt)
+    helper = rank in helpers
+    no, np_ = wid[rank], wid[peer]
+    o0 = 0 if heavy else wh
+    cols = {"le": (wh, we), "lh": (0, wh)}
+    cols["rp"], cols["ro"] = ((wh, we), (0, wa)) if heavy else ((0, wa), (wh, we))
+    nrp, nro = cols["rp"][1], cols["ro"][1]
     pc = cores[peer]
-    on = topo.mask(core, pc) & ~topo.mask(core, relays["cable"])
-    mine, his = plan(rank), plan(mate)
-    x_need = sum(_bits(topo.mask(p[4], core)) for p in his if p[1] != "y")
-    y_need = sum(_bits(topo.mask(p[4], core)) for p in his if p[1] == "y")
-    p_need = 2 * _bits(on)
+    on = topo.mask(core, pc)
+    inner = on & ~topo.mask(core, relays["cable"])
+    mine = plan(rank)
 
-    g.sync.dma_start(T.xb[:, 0:4 * nl], T.x[:, 0:4 * nl]).then_inc(s.xl, 16)
-    g.sync.dma_start(T.wb[:, 0:8 * TW], T.w1[:, :]).then_inc(s.wl, 16)
-    g.sync.dma_start(T.wb[:, 8 * TW:12 * TW], T.w2[:, :]).then_inc(s.wl, 16)
+    def need(asem):
+        return sum(_bits(topo.mask(p[3], core)) for r in range(len(cores)) for p in plan(r) if rank in p[6] and p[7] == asem)
 
-    n = 0
+    def load_x():
+        g.sync.dma_start(T.xb[:, 0:4 * no], T.x[:, 0:4 * no]).then_inc(s.xl, 16)
+
+    if rank == hv:
+        load_x()
+    g.sync.dma_start(T.wb[:, 0:8 * TW], T.w1[:, :]).then_inc(s.w1l, 16)
+    g.sync.dma_start(T.wb[:, 8 * TW:12 * TW], T.w2[:, :]).then_inc(s.w2l, 16)
+    if rank != hv:
+        load_x()
+
+    n = [0]
+
+    def cross(kind):
+        ts = []
+        for k, a, b, relay, mask, sem, _, _ in mine:
+            if k == kind:
+                rid, pid = topo.addr(relay, core)
+                ts.append(RemoteDMATransfer(dst_ids=[DstId(rid=rid, pnc=pid)], dma_engine_mask=mask, remote_sem=T.sem[sem],
+                                            src=view(k, True, rank, a, b), dst=view(k, False, rank, a, b)))
+                n[0] += _bits(mask)
+        g.remote_dma_fused(ts, local_sem=s.sent)
+
+    def to_peer(out, in_, rsem, mask):
+        rid, pid = topo.addr(pc, core)
+        g.remote_dma(out, in_, rsem, s.sent, pid, rid, mask)
+        n[0] += _bits(mask)
+
+    if rank == hv:
+        g.wait_ge(s.xqd, 1)
+        cross("xs")
+        cross("xq")
+    g.wait_ge(s.w1q, 1)
+    cross("1s")
+    cross("1q")
+    g.wait_ge(s.w2q, 1)
+    cross("2s")
+    cross("2q")
     g.wait_ge(s.xqd, 1)
-    for i in range(len(X_CALLS)):
-        n += issue([p for p in mine if p[0] == i])
-    g.wait_ge(s.wqd, 1)
-    n += send(pc, T.pq[:, :].bitcast(dt.uint8), T.wq[:, :].bitcast(dt.uint8), s.parr, on)
-    n += send(pc, T.ps[:, :], T.ws[:, :], s.parr, on)
+    vq, vs = T.xq[:, o0:o0 + no].bitcast(dt.uint8), T.xs[:, o0:o0 + no]
+    to_peer(vq, vq, s.xparr, inner)
+    to_peer(vs, vs, s.xparr, inner)
+    if helper:
+        g.wait_ge(s.yed, 1)
+        cross("ye")
     g.wait_ge(s.ypd, 1)
-    for i in range(len(X_CALLS), len(X_CALLS) + len(Y_CALLS)):
-        n += issue([p for p in mine if p[0] == i])
-    g.wait_ge(s.sent, n)
+    to_peer(T.yl[:, 0:np_], T.yp[:, 0:np_], s.yarr, on)
+    g.wait_ge(s.sent, n[0])
 
     te = g.tensor
+    zb = {"le": (T.z0, T.z1), "lh": (T.z2, T.z3), "rp": (T.z0, T.z1), "ro": (T.z2, T.z3)}
 
-    def mm(out, n, wq, ws, i, xq, xs, start=True, stop=True):
-        a, b = TW * i, TW * i + TW
-        return te.matmul_mx(out[:, 0:n], wq[:, a:b], ws[:, a:b], xq[:, 0:n], xs[:, 0:n], start, stop)
+    def first(k, wq, ws):
+        a, m = cols[k]
+        for i in (0, 1):
+            te.matmul_mx(zb[k][i][:, 0:m], wq[:, TW * i:TW * i + TW], ws[:, TW * i:TW * i + TW],
+                         T.xq[:, a:a + m], T.xs[:, a:a + m], True, True).then_inc(T.sem["z%d" % i + k], 1)
 
+    def second(k, out, wq, ws, start, stop):
+        m = cols[k][1]
+        return te.matmul_mx(out[:, 0:m], wq[:, 2 * TW:3 * TW], ws[:, 2 * TW:3 * TW],
+                            T["hq_" + k][:, 0:m], T["hs_" + k][:, 0:m], start, stop)
+
+    te.wait_ge(s.w1q, 1)
+    te.wait_ge(s.w2q, 1)
     te.wait_ge(s.xqd, 1)
-    te.wait_ge(s.wqd, 1)
-    mm(T.zl0, nl, T.wq, T.ws, 0, T.xq, T.xs).then_inc(s.z0lo, 1)
-    mm(T.zl1, nl, T.wq, T.ws, 1, T.xq, T.xs).then_inc(s.z1lo, 1)
-    te.wait_ge(s.qlo, 1)
-    mm(T.yloc, nl, T.wq, T.ws, 2, T.hq_lo, T.hs_lo, True, False)
-    te.wait_ge(s.xarr, x_need)
-    mm(T.zo0, nr, T.wq, T.ws, 0, T.rq, T.rs).then_inc(s.z0ro, 1)
-    mm(T.zo1, nr, T.wq, T.ws, 1, T.rq, T.rs).then_inc(s.z1ro, 1)
-    te.wait_ge(s.parr, p_need)
-    mm(T.zp0, nr, T.pq, T.ps, 0, T.rq, T.rs).then_inc(s.z0rp, 1)
-    mm(T.zp1, nr, T.pq, T.ps, 1, T.rq, T.rs).then_inc(s.z1rp, 1)
-    te.wait_ge(s.qro, 1)
-    mm(T.yrem, nr, T.wq, T.ws, 2, T.hq_ro, T.hs_ro, True, False)
+    te.wait_ge(s.xparr, 2 * _bits(inner))
+    first("le", T.wq, T.ws)
+    te.wait_ge(s.qle, 1)
+    if heavy:
+        second("le", T.yle, T.wq, T.ws, True, True).then_inc(s.yle, 1)
+    else:
+        second("le", T.yle, T.wq, T.ws, True, False)
+    if helper:
+        te.wait_ge(s.xearr, need("xearr"))
+    first("lh", T.wq, T.ws)
+    te.wait_ge(s.qlh, 1)
+    second("lh", T.ylh, T.wq, T.ws, True, True).then_inc(s.ylh, 1)
+    te.wait_ge(s.w1arr, need("w1arr"))
+    first("rp", T.rq, T.rs)
+    first("ro", T.rq, T.rs)
+    te.wait_ge(s.w2arr, need("w2arr"))
     te.wait_ge(s.qrp, 1)
-    mm(T.yrem, nr, T.pq, T.ps, 2, T.hq_rp, T.hs_rp, False, True).then_inc(s.yrd, 1)
-    mm(T.zl0, nl, T.pq, T.ps, 0, T.xq, T.xs).then_inc(s.z0lp, 1)
-    mm(T.zl1, nl, T.pq, T.ps, 1, T.xq, T.xs).then_inc(s.z1lp, 1)
-    te.wait_ge(s.qlp, 1)
-    mm(T.yloc, nl, T.pq, T.ps, 2, T.hq_lp, T.hs_lp, False, True).then_inc(s.yld, 1)
+    second("rp", T.yrp, T.rq, T.rs, True, True).then_inc(s.yrp, 1)
+    te.wait_ge(s.qro, 1)
+    if heavy:
+        second("ro", T.yro, T.rq, T.rs, True, True).then_inc(s.yro, 1)
+    else:
+        second("ro", T.yle, T.rq, T.rs, False, True).then_inc(s.yro, 1)
 
     ve, sc = g.vector, g.scalar
 
-    def act_s(h, b, n, z, sem):
-        sc.activation(h[:, b:4 * n:4], z[:, 0:n], ActivationFunctionType.Relu,
-                      scale=-ALPHA if b % 2 else ALPHA).then_inc(sem, 1)
+    def act_s(k):
+        m = cols[k][1]
+        sc.wait_ge(T.sem["z0" + k], 1)
+        for b in (0, 1):
+            sc.activation(T["h_" + k][:, b:4 * m:4], zb[k][0][:, 0:m], ActivationFunctionType.Relu,
+                          scale=-ALPHA if b % 2 else ALPHA).then_inc(T.sem["as" + k], 1)
 
-    def act_v(h, b, n, z, sem):
-        ve.tensor_scalar(h[:, b:4 * n:4], z[:, 0:n], -ALPHA if b % 2 else ALPHA, 0.0,
-                         AluOpType.mult, AluOpType.max).then_inc(sem, 1)
+    def act_v(k):
+        m = cols[k][1]
+        ve.wait_ge(T.sem["z1" + k], 1)
+        for b in (2, 3):
+            ve.tensor_scalar(T["h_" + k][:, b:4 * m:4], zb[k][1][:, 0:m], -ALPHA if b % 2 else ALPHA, 0.0,
+                             AluOpType.mult, AluOpType.max).then_inc(T.sem["av" + k], 1)
+        ve.wait_ge(T.sem["as" + k], 2)
+        ve.wait_ge(T.sem["av" + k], 2)
+        ve.quantize_mx(T["hq_" + k][:, 0:m], T["hs_" + k][:, 0:m], T["h_" + k][:, 0:4 * m]).then_inc(T.sem["q" + k], 1)
 
-    def quant(k, n):
-        ve.quantize_mx(T["hq_" + k][:, 0:n], T["hs_" + k][:, 0:n], T["h_" + k][:, 0:4 * n]).then_inc(T.sem["q" + k], 1)
+    def copy(out, in_, sem):
+        sc.activation(out, in_, ActivationFunctionType.Copy).then_inc(sem, 1)
 
-    sc.wait_ge(s.z0lo, 1)
-    act_s(T.h_lo, 0, nl, T.zl0, s.aslo)
-    act_s(T.h_lo, 1, nl, T.zl0, s.aslo)
-    sc.wait_ge(s.z0ro, 1)
-    act_s(T.h_ro, 0, nr, T.zo0, s.asro)
-    act_s(T.h_ro, 1, nr, T.zo0, s.asro)
-    sc.wait_ge(s.v2s, 1)
-    act_s(T.h_ro, 2, nr, T.zo1, s.asro)
-    sc.wait_ge(s.z1rp, 1)
-    act_s(T.h_rp, 2, nr, T.zp1, s.asrp)
-    act_s(T.h_rp, 3, nr, T.zp1, s.asrp)
-    sc.wait_ge(s.yrd, 1)
-    sc.activation(T.yp[:, 0:nr], T.yrem[:, 0:nr], ActivationFunctionType.Copy).then_inc(s.ypd, 1)
-    sc.wait_ge(s.z0lp, 1)
-    act_s(T.h_lp, 0, nl, T.zl0, s.aslp)
-    act_s(T.h_lp, 1, nl, T.zl0, s.aslp)
+    act_s("le")
+    if heavy:
+        sc.wait_ge(s.yle, 1)
+        copy(T.yp[:, 0:np_], T.yle[:, 0:np_], s.ypc)
+    act_s("lh")
+    sc.wait_ge(s.ylh, 1)
+    if helper:
+        copy(T.ye[:, 0:wh - wa], T.ylh[:, wa:wh], s.yed)
+    if heavy:
+        copy(T.yo[:, 0:no], T.ylh[:, 0:no], s.yoc)
+    else:
+        copy(T.yp[:, 0:np_], T.ylh[:, 0:np_], s.ypc)
+    act_s("rp")
+    act_s("ro")
 
-    ve.wait_ge(s.xl, 16)
-    ve.quantize_mx(T.xq[:, 0:nl], T.xs[:, 0:nl], T.xb[:, 0:4 * nl]).then_inc(s.xqd, 1)
-    ve.wait_ge(s.wl, 32)
-    ve.quantize_mx(T.wq[:, :], T.ws[:, :], T.wb[:, :]).then_inc(s.wqd, 1)
-    ve.wait_ge(s.z1lo, 1)
-    act_v(T.h_lo, 2, nl, T.zl1, s.avlo)
-    act_v(T.h_lo, 3, nl, T.zl1, s.avlo)
-    ve.wait_ge(s.aslo, 2)
-    ve.wait_ge(s.avlo, 2)
-    quant("lo", nl)
-    ve.wait_ge(s.z1ro, 1)
-    act_v(T.h_ro, 3, nr, T.zo1, s.v2s)
-    ve.wait_ge(s.z0rp, 1)
-    act_v(T.h_rp, 0, nr, T.zp0, s.avrp)
-    ve.wait_ge(s.asro, 3)
-    ve.wait_ge(s.v2s, 1)
-    quant("ro", nr)
-    act_v(T.h_rp, 1, nr, T.zp0, s.avrp)
-    ve.wait_ge(s.asrp, 2)
-    ve.wait_ge(s.avrp, 2)
-    quant("rp", nr)
-    ve.wait_ge(s.z1lp, 1)
-    act_v(T.h_lp, 2, nl, T.zl1, s.avlp)
-    act_v(T.h_lp, 3, nl, T.zl1, s.avlp)
-    ve.wait_ge(s.aslp, 2)
-    ve.wait_ge(s.avlp, 2)
-    quant("lp", nl)
-    ve.wait_ge(s.yld, 1)
-    ve.wait_ge(s.yarr, y_need)
-    ve.tensor_tensor(T.yo[:, 0:nl], T.yloc[:, 0:nl], T.yl[:, 0:nl], AluOpType.add).then_inc(s.yod, 1)
+    def quant_x():
+        ve.wait_ge(s.xl, 16)
+        ve.quantize_mx(T.xq[:, o0:o0 + no], T.xs[:, o0:o0 + no], T.xb[:, 0:4 * no]).then_inc(s.xqd, 1)
+
+    def add(out, a, b, sem):
+        ve.tensor_tensor(out, a, b, AluOpType.add).then_inc(sem, 1)
+
+    if rank == hv:
+        quant_x()
+    ve.wait_ge(s.w1l, 16)
+    ve.quantize_mx(T.wq[:, 0:2 * TW], T.ws[:, 0:2 * TW], T.wb[:, 0:8 * TW]).then_inc(s.w1q, 1)
+    ve.wait_ge(s.w2l, 16)
+    ve.quantize_mx(T.wq[:, 2 * TW:3 * TW], T.ws[:, 2 * TW:3 * TW], T.wb[:, 8 * TW:12 * TW]).then_inc(s.w2q, 1)
+    if rank != hv:
+        quant_x()
+    act_v("le")
+    act_v("lh")
+    act_v("rp")
+    ve.wait_ge(s.yrp, 1)
+    ve.wait_ge(s.ypc, 1)
+    add(T.yp[:, 0:nrp], T.yrp[:, 0:nrp], T.yp[:, 0:nrp], s.ypd)
+    act_v("ro")
+    ve.wait_ge(s.yro, 1)
+    if heavy:
+        ve.wait_ge(s.yoc, 1)
+        add(T.yo[:, 0:nro], T.yro[:, 0:nro], T.yo[:, 0:nro], s.v1)
+        ve.wait_ge(s.v1, 1)
+        ve.wait_ge(s.yarr, _bits(on))
+        add(T.yo[:, 0:no], T.yo[:, 0:no], T.yl[:, 0:no], s.yod)
+        if rank == hv:
+            ve.wait_ge(s.yod, 1)
+            ve.wait_ge(s.e0arr, need("e0arr"))
+            add(T.yo[:, wa:wh], T.yo[:, wa:wh], T.e0[:, 0:wh - wa], s.v2)
+            ve.wait_ge(s.v2, 1)
+            ve.wait_ge(s.e1arr, need("e1arr"))
+            add(T.yo[:, wa:wh], T.yo[:, wa:wh], T.e1[:, 0:wh - wa], s.yod2)
+    else:
+        ve.wait_ge(s.yarr, _bits(on))
+        add(T.yo[:, 0:no], T.yle[:, 0:no], T.yl[:, 0:no], s.yod)
 
     g.sync.wait_ge(s.yod, 1)
-    g.sync.dma_start(T.y[:, 0:nl], T.yo[:, 0:nl]).then_inc(s.st, 16)
+    m = wa if rank == hv else no
+    g.sync.dma_start(T.y[:, 0:m], T.yo[:, 0:m]).then_inc(s.st, 16)
+    if rank == hv:
+        sc.wait_ge(s.yod2, 1)
+        sc.dma_start(T.y[:, wa:wh], T.yo[:, wa:wh]).then_inc(s.st2, 16)
+        sc.wait_ge(s.st2, 16)
     g.sync.wait_ge(s.st, 16)

from concourse.bass import DstId, RemoteDMATransfer
from concourse.mybir import dt, AluOpType, ActivationFunctionType

WX = 192
WA = 384
WW = 384
TW = 128
NCORES = 512
ALPHA = 0.043

SCRATCH = {
    "xb": ("sbuf", [128, 4 * WX], "bfloat16"),
    "wb": ("sbuf", [128, 4 * WW], "bfloat16"),
    "xq": ("sbuf", [128, WA], "float8_e4m3fn_x4"), "xs": ("sbuf", [128, WA], "uint8"),
    "wq": ("sbuf", [128, WW], "float8_e4m3fn_x4"), "ws": ("sbuf", [128, WW], "uint8"),
    "rq": ("sbuf", [128, WW], "float8_e4m3fn_x4"), "rs": ("sbuf", [128, WW], "uint8"),
    "yp": ("sbuf", [128, WX], "float32"),
    "yl": ("sbuf", [128, WX], "float32"),
    "ye": ("sbuf", [128, WX], "float32"),
    "e0": ("sbuf", [128, WX], "float32"),
    "e1": ("sbuf", [128, WX], "float32"),
    "yo": ("sbuf", [128, WX], "float32"),
}
GROUPS = ("le", "lh", "rp", "ro")
for _k in GROUPS:
    SCRATCH["h_" + _k] = ("sbuf", [128, 4 * WX], "bfloat16")
    SCRATCH["hq_" + _k] = ("sbuf", [128, WX], "float8_e4m3fn_x4")
    SCRATCH["hs_" + _k] = ("sbuf", [128, WX], "uint8")
for _k in ("z0", "z1", "z2", "z3", "yle", "ylh", "yrp", "yro"):
    SCRATCH[_k] = ("psum", [128, 512], "float32")

SEMAPHORES = ["xl", "w1l", "w2l", "xqd", "w1q", "w2q", "sent", "xearr", "w1arr", "w2arr", "xparr", "yarr", "e0arr", "e1arr",
              "yed", "ypc", "yoc", "ypd", "v1", "v2", "v3", "yod", "yod2", "st", "st2"]
SEMAPHORES += ["r%d" % _k for _k in range(12)]
for _k in GROUPS:
    SEMAPHORES += ["z0" + _k, "z1" + _k, "av" + _k, "as" + _k, "q" + _k, "y" + _k]


def _bits(mask):
    return bin(mask).count("1")


def _split(mask, k):
    e = [1 << i for i in range(16) if mask >> i & 1]
    return [sum(e[j::k]) for j in range(k)]


def _roles(T, topo):
    cores = list(T.cores)
    lanes = []
    for c in cores:
        peer = [k for k, d in enumerate(cores) if d != c and topo.host(d) == topo.host(c)][0]
        mate = [k for k, d in enumerate(cores) if topo.host(d) != topo.host(c) and topo.die(d) == topo.die(c)][0]
        near = [d for d in range(NCORES) if topo.chip(d) == topo.chip(c) and topo.die(d) == topo.die(c)
                and topo.host(d) not in (topo.host(c), topo.host(cores[mate]))]
        cable = [d for d in near if topo.rack(topo.host(d)) != topo.rack(topo.host(c))][0]
        switch = [d for d in near if topo.rack(topo.host(d)) == topo.rack(topo.host(c))][-1]
        lanes.append((peer, mate, {"cable": cable, "switch": switch}))
    return lanes


def rank_program(g, core, T, topo):
    wid = T.tables["WID"]
    cores = list(T.cores)
    if topo.chip(core) not in [topo.chip(c) for c in cores]:
        return
    lanes = _roles(T, topo)
    s = T.sem
    hv = max(range(len(cores)), key=lambda k: wid[k])
    lt = lanes[hv][1]
    wa, wh = wid[lt], wid[hv]
    we = wid[lanes[hv][0]]
    helpers = (lt, lanes[lt][0])

    def view(kind, src, r, a, b):
        if kind == "xq":
            return T.xq[:, a:b].bitcast(dt.uint8)
        if kind == "xs":
            return T.xs[:, a:b]
        if kind[1] == "q":
            return (T.wq if src else T.rq)[:, a:b].bitcast(dt.uint8)
        if kind[1] == "s":
            return (T.ws if src else T.rs)[:, a:b]
        return (T.ye if src else T.e0 if r == lt else T.e1)[:, a:b]

    def plan(r):
        def halves(a, b):
            m = (a + b) // 2
            return [(a, m, "cable"), (m, b, "switch")]
        calls = []
        if r == hv:
            calls += [(k, halves(wa, wh), helpers, "xearr") for k in ("xs", "xq")]
        mate = (lanes[r][1],)
        calls += [(k, halves(0, 2 * TW), mate, "w1arr") for k in ("1s", "1q")]
        calls += [(k, halves(2 * TW, 3 * TW), mate, "w2arr") for k in ("2s", "2q")]
        if r in helpers:
            calls += [("ye", halves(0, wh - wa), (hv,), "e0arr" if r == lt else "e1arr")]
        out = []
        for kind, hs, to, asem in calls:
            for j, (a, b, way) in enumerate(hs):
                relay = lanes[r][2][way]
                out.append((kind, a, b, relay, _split(topo.mask(cores[r], relay), len(hs))[j], "r%d" % len(out), to, asem))
        return out

    rank = T.rank_of(core)
    if rank is None:
        n = 0
        for r in range(len(cores)):
            for kind, a, b, relay, mask, sem, to, asem in plan(r):
                if relay == core:
                    g.wait_ge(T.sem[sem], _bits(mask))
                    v = view(kind, False, r, a, b)
                    out = topo.mask(core, cores[to[0]])
                    if len(to) == 1:
                        rid, pid = topo.addr(cores[to[0]], core)
                        g.remote_dma(v, v, T.sem[asem], s.sent, pid, rid, out)
                    else:
                        ids = []
                        for k in to:
                            rid, pid = topo.addr(cores[k], core)
                            ids.append(DstId(rid=rid, pnc=pid))
                        g.remote_dma_fused([RemoteDMATransfer(dst_ids=ids, dma_engine_mask=out, remote_sem=T.sem[asem],
                                                              srcs=[v], dsts=[v for k in to])], local_sem=s.sent)
                    n += _bits(out)
        if n:
            g.wait_ge(s.sent, n)
        return

    peer, mate, relays = lanes[rank]
    heavy = rank in (hv, lt)
    helper = rank in helpers
    no, np_ = wid[rank], wid[peer]
    o0 = 0 if heavy else wh
    cols = {"le": (wh, we), "lh": (0, wh)}
    cols["rp"], cols["ro"] = ((wh, we), (0, wa)) if heavy else ((0, wa), (wh, we))
    nrp, nro = cols["rp"][1], cols["ro"][1]
    pc = cores[peer]
    on = topo.mask(core, pc)
    inner = on & ~topo.mask(core, relays["cable"])
    mine = plan(rank)

    def need(asem):
        return sum(_bits(topo.mask(p[3], core)) for r in range(len(cores)) for p in plan(r) if rank in p[6] and p[7] == asem)

    def load_x():
        g.sync.dma_start(T.xb[:, 0:4 * no], T.x[:, 0:4 * no]).then_inc(s.xl, 16)

    if rank == hv:
        load_x()
    g.sync.dma_start(T.wb[:, 0:8 * TW], T.w1[:, :]).then_inc(s.w1l, 16)
    g.sync.dma_start(T.wb[:, 8 * TW:12 * TW], T.w2[:, :]).then_inc(s.w2l, 16)
    if rank != hv:
        load_x()

    n = [0]

    def cross(kind):
        ts = []
        for k, a, b, relay, mask, sem, _, _ in mine:
            if k == kind:
                rid, pid = topo.addr(relay, core)
                ts.append(RemoteDMATransfer(dst_ids=[DstId(rid=rid, pnc=pid)], dma_engine_mask=mask, remote_sem=T.sem[sem],
                                            src=view(k, True, rank, a, b), dst=view(k, False, rank, a, b)))
                n[0] += _bits(mask)
        g.remote_dma_fused(ts, local_sem=s.sent)

    def to_peer(out, in_, rsem, mask):
        rid, pid = topo.addr(pc, core)
        g.remote_dma(out, in_, rsem, s.sent, pid, rid, mask)
        n[0] += _bits(mask)

    if rank == hv:
        g.wait_ge(s.xqd, 1)
        cross("xs")
        cross("xq")
    g.wait_ge(s.w1q, 1)
    cross("1s")
    cross("1q")
    g.wait_ge(s.w2q, 1)
    cross("2s")
    cross("2q")
    g.wait_ge(s.xqd, 1)
    vq, vs = T.xq[:, o0:o0 + no].bitcast(dt.uint8), T.xs[:, o0:o0 + no]
    to_peer(vq, vq, s.xparr, inner)
    to_peer(vs, vs, s.xparr, inner)
    if helper:
        g.wait_ge(s.yed, 1)
        cross("ye")
    g.wait_ge(s.ypd, 1)
    to_peer(T.yl[:, 0:np_], T.yp[:, 0:np_], s.yarr, on)
    g.wait_ge(s.sent, n[0])

    te = g.tensor
    zb = {"le": (T.z0, T.z1), "lh": (T.z2, T.z3), "rp": (T.z0, T.z1), "ro": (T.z2, T.z3)}

    def first(k, wq, ws):
        a, m = cols[k]
        for i in (0, 1):
            te.matmul_mx(zb[k][i][:, 0:m], wq[:, TW * i:TW * i + TW], ws[:, TW * i:TW * i + TW],
                         T.xq[:, a:a + m], T.xs[:, a:a + m], True, True).then_inc(T.sem["z%d" % i + k], 1)

    def second(k, out, wq, ws, start, stop):
        m = cols[k][1]
        return te.matmul_mx(out[:, 0:m], wq[:, 2 * TW:3 * TW], ws[:, 2 * TW:3 * TW],
                            T["hq_" + k][:, 0:m], T["hs_" + k][:, 0:m], start, stop)

    te.wait_ge(s.w1q, 1)
    te.wait_ge(s.w2q, 1)
    te.wait_ge(s.xqd, 1)
    te.wait_ge(s.xparr, 2 * _bits(inner))
    first("le", T.wq, T.ws)
    te.wait_ge(s.qle, 1)
    if heavy:
        second("le", T.yle, T.wq, T.ws, True, True).then_inc(s.yle, 1)
    else:
        second("le", T.yle, T.wq, T.ws, True, False)
    if helper:
        te.wait_ge(s.xearr, need("xearr"))
    first("lh", T.wq, T.ws)
    te.wait_ge(s.qlh, 1)
    second("lh", T.ylh, T.wq, T.ws, True, True).then_inc(s.ylh, 1)
    te.wait_ge(s.w1arr, need("w1arr"))
    first("rp", T.rq, T.rs)
    first("ro", T.rq, T.rs)
    te.wait_ge(s.w2arr, need("w2arr"))
    te.wait_ge(s.qrp, 1)
    second("rp", T.yrp, T.rq, T.rs, True, True).then_inc(s.yrp, 1)
    te.wait_ge(s.qro, 1)
    if heavy:
        second("ro", T.yro, T.rq, T.rs, True, True).then_inc(s.yro, 1)
    else:
        second("ro", T.yle, T.rq, T.rs, False, True).then_inc(s.yro, 1)

    ve, sc = g.vector, g.scalar

    def act_s(k):
        m = cols[k][1]
        sc.wait_ge(T.sem["z0" + k], 1)
        for b in (0, 1):
            sc.activation(T["h_" + k][:, b:4 * m:4], zb[k][0][:, 0:m], ActivationFunctionType.Relu,
                          scale=-ALPHA if b % 2 else ALPHA).then_inc(T.sem["as" + k], 1)

    def act_v(k):
        m = cols[k][1]
        ve.wait_ge(T.sem["z1" + k], 1)
        for b in (2, 3):
            ve.tensor_scalar(T["h_" + k][:, b:4 * m:4], zb[k][1][:, 0:m], -ALPHA if b % 2 else ALPHA, 0.0,
                             AluOpType.mult, AluOpType.max).then_inc(T.sem["av" + k], 1)
        ve.wait_ge(T.sem["as" + k], 2)
        ve.wait_ge(T.sem["av" + k], 2)
        ve.quantize_mx(T["hq_" + k][:, 0:m], T["hs_" + k][:, 0:m], T["h_" + k][:, 0:4 * m]).then_inc(T.sem["q" + k], 1)

    def copy(out, in_, sem):
        sc.activation(out, in_, ActivationFunctionType.Copy).then_inc(sem, 1)

    act_s("le")
    if heavy:
        sc.wait_ge(s.yle, 1)
        copy(T.yp[:, 0:np_], T.yle[:, 0:np_], s.ypc)
    act_s("lh")
    sc.wait_ge(s.ylh, 1)
    if helper:
        copy(T.ye[:, 0:wh - wa], T.ylh[:, wa:wh], s.yed)
    if heavy:
        copy(T.yo[:, 0:no], T.ylh[:, 0:no], s.yoc)
    else:
        copy(T.yp[:, 0:np_], T.ylh[:, 0:np_], s.ypc)
    act_s("rp")
    act_s("ro")

    def quant_x():
        ve.wait_ge(s.xl, 16)
        ve.quantize_mx(T.xq[:, o0:o0 + no], T.xs[:, o0:o0 + no], T.xb[:, 0:4 * no]).then_inc(s.xqd, 1)

    def add(out, a, b, sem):
        ve.tensor_tensor(out, a, b, AluOpType.add).then_inc(sem, 1)

    if rank == hv:
        quant_x()
    ve.wait_ge(s.w1l, 16)
    ve.quantize_mx(T.wq[:, 0:2 * TW], T.ws[:, 0:2 * TW], T.wb[:, 0:8 * TW]).then_inc(s.w1q, 1)
    ve.wait_ge(s.w2l, 16)
    ve.quantize_mx(T.wq[:, 2 * TW:3 * TW], T.ws[:, 2 * TW:3 * TW], T.wb[:, 8 * TW:12 * TW]).then_inc(s.w2q, 1)
    if rank != hv:
        quant_x()
    act_v("le")
    act_v("lh")
    act_v("rp")
    ve.wait_ge(s.yrp, 1)
    ve.wait_ge(s.ypc, 1)
    add(T.yp[:, 0:nrp], T.yrp[:, 0:nrp], T.yp[:, 0:nrp], s.ypd)
    act_v("ro")
    ve.wait_ge(s.yro, 1)
    if heavy:
        ve.wait_ge(s.yoc, 1)
        add(T.yo[:, 0:nro], T.yro[:, 0:nro], T.yo[:, 0:nro], s.v1)
        ve.wait_ge(s.v1, 1)
        ve.wait_ge(s.yarr, _bits(on))
        add(T.yo[:, 0:no], T.yo[:, 0:no], T.yl[:, 0:no], s.yod)
        if rank == hv:
            ve.wait_ge(s.yod, 1)
            ve.wait_ge(s.e0arr, need("e0arr"))
            add(T.yo[:, wa:wh], T.yo[:, wa:wh], T.e0[:, 0:wh - wa], s.v2)
            ve.wait_ge(s.v2, 1)
            ve.wait_ge(s.e1arr, need("e1arr"))
            add(T.yo[:, wa:wh], T.yo[:, wa:wh], T.e1[:, 0:wh - wa], s.yod2)
    else:
        ve.wait_ge(s.yarr, _bits(on))
        add(T.yo[:, 0:no], T.yle[:, 0:no], T.yl[:, 0:no], s.yod)

    g.sync.wait_ge(s.yod, 1)
    m = wa if rank == hv else no
    g.sync.dma_start(T.y[:, 0:m], T.yo[:, 0:m]).then_inc(s.st, 16)
    if rank == hv:
        sc.wait_ge(s.yod2, 1)
        sc.dma_start(T.y[:, wa:wh], T.yo[:, wa:wh]).then_inc(s.st2, 16)
        sc.wait_ge(s.st2, 16)
    g.sync.wait_ge(s.st, 16)
